import numpy as np
import ml_dtypes


def mxq(x, axis, fmt="e4m3"):
    dtype, down = {"e4m3": (ml_dtypes.float8_e4m3fn, 7), "e5m2": (ml_dtypes.float8_e5m2, 14)}[fmt]
    v = np.moveaxis(np.asarray(x, np.float32).astype(ml_dtypes.bfloat16).astype(np.float64), axis, -1)
    blocks = v.reshape(v.shape[:-1] + (-1, 32))
    amax = np.abs(blocks).max(-1, keepdims=True)
    byte = np.maximum(np.where(amax > 0, np.frexp(amax)[1] - 1 + 127, 0) - down, 1)
    scale = np.exp2(byte - 127.0)
    codes = (blocks / scale).astype(np.float32).astype(dtype).astype(np.float64)
    return np.moveaxis((codes * scale).reshape(v.shape), -1, axis)


WIDE = False


def mx_kscale(k):
    if not WIDE:
        return np.ones(k)
    levels = np.array([10, -10, 5, -5, 0])
    if k % 512:
        return np.exp2(np.random.permutation(np.resize(levels, k // 32))).repeat(32)
    a = np.empty((k // 512, 16))
    for p in range(k // 512):
        a[p, :8] = np.random.permutation(np.resize(levels, 8))
        for g in range(8):
            far = levels[np.abs(levels - a[p, g]) >= 10]
            a[p, g + 8] = far[np.random.randint(len(far))]
    return np.exp2(a.ravel()).repeat(32)


def f64(x):
    return np.asarray(x).astype(np.float64)


def striped(idx):
    return np.tile(np.asarray(idx).reshape(-1, 16).T, (8, 1)).astype(np.uint16)


def unstriped(offs):
    return offs[:16].T.reshape(-1).astype(np.int64)


E2M1 = np.array([0.0, 0.5, 1.0, 1.5, 2.0, 3.0, 4.0, 6.0, -0.0, -0.5, -1.0, -1.5, -2.0, -3.0, -4.0, -6.0])


def pack_weight(w, fmt):
    k, n = w.shape
    w = f64(np.asarray(w, np.float32).astype(ml_dtypes.bfloat16)).reshape(k // 32, 32, n)
    amax = np.abs(w).max(1)
    if fmt == "e4m3":
        byte = np.frexp(amax)[1] - 1 + 127 - 7
    else:
        mant, ex = np.frexp(amax / 6.0)
        byte = np.where(mant > 0.5, ex, ex - 1) + 127
    byte = np.clip(np.where(amax > 0, byte, 1), 1, 254)
    scaled = (w * np.exp2(127.0 - byte)[:, None, :]).reshape(k, n).astype(np.float32)
    by_word = np.ascontiguousarray(scaled.reshape(k // 512, 128, 4, n).transpose(0, 1, 3, 2))
    if fmt == "e4m3":
        words = by_word.astype(ml_dtypes.float8_e4m3fn).view(np.uint8)
    else:
        c = by_word.astype(ml_dtypes.float4_e2m1fn).view(np.uint8) & 0xF
        words = (c[..., 0::2] | (c[..., 1::2] << 4)).reshape(k // 512, 128, 2 * n)
    return np.ascontiguousarray(words), np.ascontiguousarray(byte.astype(np.uint8).reshape(k // 512, 16, n))


def unpack_weight(words, scales, fmt):
    g, _, n = scales.shape
    words = np.ascontiguousarray(words).reshape(g, 128, n, -1)
    if fmt == "e4m3":
        vals = words.view(ml_dtypes.float8_e4m3fn).astype(np.float64)
    else:
        nib = np.empty((g, 128, n, 4), np.uint8)
        nib[..., 0::2] = words & 0xF
        nib[..., 1::2] = words >> 4
        vals = E2M1[nib]
    vals = vals * np.repeat(np.exp2(scales.astype(np.float64) - 127.0), 8, axis=1)[..., None]
    return vals.transpose(0, 1, 3, 2).reshape(g * 512, n)


def bf(x):
    return np.asarray(x, np.float32).astype(ml_dtypes.bfloat16)


def planes(Y):
    r, m = Y.shape
    b = f64(bf(Y)).reshape(r // 32, 32, m)
    amax = np.abs(b).max(1)
    byte = np.clip(np.where(amax > 0, np.frexp(amax)[1] - 1 + 127 - 7, 1), 1, 254)
    codes = (b * np.exp2(127.0 - byte)[:, None, :]).reshape(r, m).astype(np.float32).astype(ml_dtypes.float8_e4m3fn).view(np.uint8)
    words = codes.reshape(r // 512, 128, 4, m).transpose(0, 1, 3, 2)
    return np.ascontiguousarray(words), np.ascontiguousarray(byte.astype(np.uint8).reshape(r // 512, 16, m))


K, T, J, N = 1024, 2048, 512, 512


def setup_inputs():
    n = np.random.standard_normal
    idx = np.random.permutation(T)[:J]
    fk = mx_kscale(K)
    wap = pack_weight(n((K, N)) * 1 / np.sqrt(K) * fk[:, None], "e2m1")
    wbp = pack_weight(n((K, N)) * 1 / np.sqrt(K) * fk[:, None], "e4m3")
    return {
        "xq": (n((K, T)) / fk[:, None]).astype(np.float32),
        "wa_words": wap[0],
        "wa_scales": wap[1],
        "wb_words": wbp[0],
        "wb_scales": wbp[1],
        "ga": (np.random.uniform(0.4, 1.2, (1, J))).astype(np.float32),
        "offs": striped(idx),
    }


def reference(xq, wa_words, wa_scales, wb_words, wb_scales, ga, offs):
    idx = unstriped(offs)
    wau = unpack_weight(wa_words, wa_scales, "e2m1")
    wbu = unpack_weight(wb_words, wb_scales, "e4m3")
    xqidxq = mxq(f64(xq)[:, idx], 0, "e4m3")
    p = wau.T @ xqidxq
    q = wbu.T @ xqidxq
    y = f64(ga) * (0.5 * (p + q) - 0.25 * np.abs(p - q))
    words, scales = planes(y)
    return y, words, scales

@@ -1,0 +1,206 @@
+from contextlib import ExitStack
+
+import concourse.mybir as mybir
+from concourse.masks import make_identity
+
+K, T, J, N = 1024, 2048, 512, 512
+FLOPS = 2 * 2 * K * J * N
+
+F32 = mybir.dt.float32
+BF16 = mybir.dt.bfloat16
+I32 = mybir.dt.int32
+U32 = mybir.dt.uint32
+U16 = mybir.dt.uint16
+U8 = mybir.dt.uint8
+FP8X4 = mybir.dt.float8_e4m3fn_x4
+FP4X4 = mybir.dt.float4_e2m1fn_x4
+ALU = mybir.AluOpType
+COPY = mybir.ActivationFunctionType.Copy
+
+P = 128
+PACK = 4
+PASSES = K // (P * PACK)
+CH = 128
+CHUNKS = J // CH
+B_ROW = 4
+
+
+def tile_list_experts_disagreement_pl_kernel(
+    tc, xq, wa_words, wa_scales, wb_words, wb_scales, ga, offs, out_0, out_1, out_2
+):
+    nc = tc.nc
+    with ExitStack() as ctx:
+        keep = ctx.enter_context(tc.tile_pool(name="keep", bufs=1))
+        psum = ctx.enter_context(tc.psum_pool(name="psum", bufs=1))
+
+        x_rows = xq.rearrange("(z p t) c -> z t p c", p=P, t=PACK)
+        x_sb = [[keep.tile([P, T], F32, name="x%d%d" % (z, t)) for t in range(PACK)] for z in range(PASSES)]
+        offsets = keep.tile([P, J // 16], U16, name="offsets")
+        wa_raw = keep.tile([P, PASSES, N], U16, name="wa_raw")
+        wb_raw = keep.tile([P, PASSES, N], U32, name="wb_raw")
+        ws_raw = keep.tile([P, PASSES, N], U8, name="ws_raw")
+        ga_col = keep.tile([P, PACK], F32, name="ga_col")
+        ident = keep.tile([P, P], F32, name="ident")
+
+        nc.vector.memset(ws_raw[:].bitcast(I32), 0)
+        make_identity(nc, ident[:])
+        small = [(offsets[:], offs), (ga_col[:], ga[0].rearrange("(p c) -> p c", c=PACK))]
+        for quad in range(4):
+            for row0, src in ((0, wa_scales), (B_ROW, wb_scales)):
+                small.append((
+                    ws_raw[32 * quad + row0 : 32 * quad + row0 + 4].bitcast(I32),
+                    src[:, 4 * quad : 4 * quad + 4, :].rearrange("z q c -> q z c").bitcast(I32),
+                ))
+        big = [(x_sb[z][t][:], x_rows[z, t]) for z in range(PASSES) for t in range(PACK)]
+        big[6:6] = [
+            (wb_raw[:].bitcast(I32), wb_words.rearrange("z p c r -> p z (c r)").bitcast(I32)),
+            (wa_raw[:].bitcast(I32), wa_words.rearrange("z p b -> p z b").bitcast(I32)),
+        ]
+        for i, (dst, src) in enumerate(big):
+            nc.sync.dma_start(dst, src)
+            for dst, src in small[2 * i : 2 * i + 2]:
+                nc.sync.dma_start(dst, src)
+
+        g_bank = psum.tile([P, PACK, P], F32, name="g_bank", tag="p%d" % (CHUNKS - 1))
+        for c in range(PACK):
+            nc.tensor.transpose(g_bank[:, c, :], ga_col[:, c : c + 1].to_broadcast([P, P]), ident[:])
+        g4 = keep.tile([P, J], F32, name="g4")
+        nc.vector.tensor_scalar(
+            g4[:].rearrange("p (m c) -> p m c", c=PACK), g_bank[:].rearrange("p c m -> p m c"), 0.25, None, ALU.mult
+        )
+
+        wa = keep.tile([P, PASSES, N], U16, name="wa", align_bytes=64)
+        wb = keep.tile([P, PASSES, N], U32, name="wb", align_bytes=64)
+        ws = keep.tile([P, PASSES, N], U8, name="ws", align_bytes=64)
+        nc.vector.tensor_copy(
+            ws[:].rearrange("p z (t g i) -> p z g t i", t=PACK, i=16),
+            ws_raw[:].rearrange("p z (g i t) -> p z g t i", t=PACK, i=16),
+        )
+        for z in range(PASSES):
+            nc.vector.tensor_copy(
+                wb[:, z, :].rearrange("p (t g i) -> p g t i", t=PACK, i=4),
+                wb_raw[:, z, :].rearrange("p (g i t) -> p g t i", t=PACK, i=4),
+            )
+            nc.vector.tensor_copy(
+                wa[:, z, :].rearrange("p (t g i) -> p g t i", t=PACK, i=8),
+                wa_raw[:, z, :].rearrange("p (g i t) -> p g t i", t=PACK, i=8),
+            )
+
+        def weave(dst, src):
+            nc.vector.tensor_copy(
+                dst.rearrange("p (c i t) -> p c t i", t=PACK, i=4), src.rearrange("p t (c i) -> p c t i", i=4)
+            )
+
+        p_bank = [psum.tile([P, PACK, CH], F32, name="p%d" % c, tag="p%d" % c) for c in range(CHUNKS)]
+        q_bank = [psum.tile([P, PACK, CH], F32, name="q%d" % c, tag="q%d" % c) for c in range(CHUNKS)]
+
+        def products(z, c, codes, scales):
+            for bank, w, fmt, row0 in ((q_bank[c], wb, FP8X4, B_ROW), (p_bank[c], wa, FP4X4, 0)):
+                for t in range(PACK):
+                    cols = slice(t * P, (t + 1) * P)
+                    nc.tensor.matmul_mx(
+                        out=bank[:, t, :],
+                        lhsT=w[:, z, cols].bitcast(fmt),
+                        lhsT_scale=ws[row0:P, z, cols],
+                        rhs=codes.bitcast(FP8X4),
+                        rhs_scale=scales,
+                        start=(z == 0 and t == 0),
+                        stop=(z == PASSES - 1 and t == PACK - 1),
+                    )
+
+        xg0 = keep.tile([P, PACK, J], BF16, name="xg0")
+        for t in range(PACK):
+            nc.scalar.activation(xg0[:, t, :], x_sb[0][t][:].indirect(offsets[:]), COPY)
+        xw0 = keep.tile([P, J * PACK], BF16, name="xw0", align_bytes=64)
+        weave(xw0[:], xg0[:])
+        xc0 = keep.tile([P, J], U32, name="xc0", align_bytes=64)
+        xs0 = keep.tile([P, J], U8, name="xs0", align_bytes=64)
+        nc.vector.quantize_mx(out=xc0[:].bitcast(FP8X4), scales=xs0[:], in_=xw0[:])
+        for c in range(CHUNKS):
+            cols = slice(c * CH, (c + 1) * CH)
+            products(0, c, xc0[:, cols], xs0[:, cols])
+
+        xg1 = [keep.tile([P, PACK, CH], BF16, name="xg1_%d" % c) for c in range(CHUNKS)]
+        for t in range(PACK):
+            for c in range(CHUNKS):
+                nc.scalar.activation(
+                    xg1[c][:, t, :], x_sb[1][t][:].indirect(offsets[:, c * CH // 16 : (c + 1) * CH // 16]), COPY
+                )
+        for c in range(CHUNKS):
+            xw = keep.tile([P, CH * PACK], BF16, name="xw1_%d" % c, align_bytes=64)
+            weave(xw[:], xg1[c][:])
+            xc = keep.tile([P, CH], U32, name="xc1_%d" % c, align_bytes=64)
+            xs = keep.tile([P, CH], U8, name="xs1_%d" % c, align_bytes=64)
+            nc.vector.quantize_mx(out=xc[:].bitcast(FP8X4), scales=xs[:], in_=xw[:])
+            products(1, c, xc[:], xs[:])
+
+        y_rows = out_0.rearrange("(p t) j -> p t j", t=PACK)
+        y_words = out_1[0].rearrange("p c r -> p (c r)").bitcast(I32)
+        yc = keep.tile([P, J], U32, name="yc", align_bytes=64)
+        ys = keep.tile([P, J], U8, name="ys", align_bytes=64)
+        LAST = CHUNKS - 1
+        pb = [bank[:].rearrange("p t j -> p (t j)") for bank in p_bank]
+        qb = [bank[:].rearrange("p t j -> p (t j)") for bank in q_bank]
+        qs = [keep.tile([P, PACK * CH], F32, name="qs%d" % c) for c in range(CHUNKS)]
+        low = [keep.tile([P, PACK * CH], F32, name="low%d" % c) for c in range(CHUNKS)]
+        part = [keep.tile([P, PACK * CH], F32, name="part%d" % c) for c in range(CHUNKS)]
+        u = [keep.tile([P, PACK, CH], F32, name="u%d" % c) for c in range(CHUNKS)]
+        y = [keep.tile([P, PACK, CH], F32, name="y%d" % c) for c in range(CHUNKS)]
+        yw = keep.tile([P, J * PACK], BF16, name="yw", align_bytes=64)
+
+        def step1(c):
+            nc.scalar.copy(qs[c][:], qb[c])
+            nc.vector.tensor_tensor(low[c][:], pb[c], qs[c][:], ALU.min)
+
+        def step2(c):
+            nc.vector.scalar_tensor_tensor(part[c][:], low[c][:], 2.0, pb[c], ALU.mult, ALU.add)
+
+        def step3(c):
+            nc.vector.tensor_tensor(u[c][:].rearrange("p t j -> p (t j)"), part[c][:], qb[c], ALU.add)
+
+        def gate(eng, c, a, b):
+            g = g4[:, c * CH + a : c * CH + b].unsqueeze(1).to_broadcast([P, PACK, b - a])
+            eng.tensor_tensor(y[c][:, :, a:b], u[c][:, :, a:b], g, ALU.mult)
+
+        def finish(c):
+            gate(nc.gpsimd, c, 0, CH)
+            nc.sync.dma_start(y_rows[:, :, c * CH : (c + 1) * CH], y[c][:])
+            nc.scalar.copy(
+                yw[:, c * CH * PACK : (c + 1) * CH * PACK].rearrange("p (c i t) -> p c t i", t=PACK, i=4),
+                y[c][:].rearrange("p t (c i) -> p c t i", i=4),
+            )
+
+        def planes(a, b):
+            nc.vector.quantize_mx(out=yc[:, a:b].bitcast(FP8X4), scales=ys[:, a:b], in_=yw[:, a * PACK : b * PACK])
+
+        step1(0)
+        step1(1)
+        step2(0)
+        step2(1)
+        step3(0)
+        finish(0)
+        step1(2)
+        step3(1)
+        finish(1)
+        step2(2)
+        step1(3)
+        step3(2)
+        finish(2)
+        step2(3)
+        step3(3)
+        H = CH // 2
+        j0 = LAST * CH
+        for a in (0, H):
+            gate(nc.vector, LAST, a, a + H)
+        nc.sync.dma_start(y_rows[:, :, j0:J], y[LAST][:])
+        for a in (0, H):
+            weave(yw[:, (j0 + a) * PACK : (j0 + a + H) * PACK], y[LAST][:, :, a : a + H])
+        planes(0, j0)
+        nc.sync.dma_start(y_words[:, 0:j0], yc[:, 0:j0].bitcast(I32))
+        planes(j0, J)
+        nc.sync.dma_start(y_words[:, j0:J], yc[:, j0:J].bitcast(I32))
+        for quad in range(4):
+            queue = nc.scalar if quad % 2 == 0 else nc.sync
+            queue.dma_start(
+                out_2[0, 4 * quad : 4 * quad + 4, :].bitcast(I32), ys[32 * quad : 32 * quad + 4, :].bitcast(I32)
+            )

@@ -20,8 +20,8 @@ COPY = mybir.ActivationFunctionType.Copy
 P = 128
 PACK = 4
 PASSES = K // (P * PACK)
-CH = 128
-CHUNKS = J // CH
+HALF = J // 2
+UNITS = 4
 B_ROW = 4
 
 
@@ -37,7 +37,7 @@ def tile_list_experts_disagreement_pl_kernel(
         x_sb = [[keep.tile([P, T], F32, name="x%d%d" % (z, t)) for t in range(PACK)] for z in range(PASSES)]
         offsets = keep.tile([P, J // 16], U16, name="offsets")
         wa_raw = keep.tile([P, PASSES, N], U16, name="wa_raw")
-        wb_raw = keep.tile([P, PASSES, N], U32, name="wb_raw")
+        wb_raw = [keep.tile([P, N], U32, name="wb_raw%d" % z) for z in range(PASSES)]
         ws_raw = keep.tile([P, PASSES, N], U8, name="ws_raw")
         ga_col = keep.tile([P, PACK], F32, name="ga_col")
         ident = keep.tile([P, P], F32, name="ident")
@@ -52,16 +52,15 @@ def tile_list_experts_disagreement_pl_kernel(
                     src[:, 4 * quad : 4 * quad + 4, :].rearrange("z q c -> q z c").bitcast(I32),
                 ))
         big = [(x_sb[z][t][:], x_rows[z, t]) for z in range(PASSES) for t in range(PACK)]
-        big[6:6] = [
-            (wb_raw[:].bitcast(I32), wb_words.rearrange("z p c r -> p z (c r)").bitcast(I32)),
-            (wa_raw[:].bitcast(I32), wa_words.rearrange("z p b -> p z b").bitcast(I32)),
-        ]
+        wb_load = [(wb_raw[z][:].bitcast(I32), wb_words[z].rearrange("p c r -> p (c r)").bitcast(I32)) for z in range(PASSES)]
+        wa_load = (wa_raw[:].bitcast(I32), wa_words.rearrange("z p b -> p z b").bitcast(I32))
+        big = big[:6] + [wa_load, big[6], wb_load[0], big[7], wb_load[1]]
         for i, (dst, src) in enumerate(big):
             nc.sync.dma_start(dst, src)
             for dst, src in small[2 * i : 2 * i + 2]:
                 nc.sync.dma_start(dst, src)
 
-        g_bank = psum.tile([P, PACK, P], F32, name="g_bank", tag="p%d" % (CHUNKS - 1))
+        g_bank = psum.tile([P, PACK, P], F32, name="g_bank", tag="q%d" % (UNITS - 1))
         for c in range(PACK):
             nc.tensor.transpose(g_bank[:, c, :], ga_col[:, c : c + 1].to_broadcast([P, P]), ident[:])
         g4 = keep.tile([P, J], F32, name="g4")
@@ -70,7 +69,7 @@ def tile_list_experts_disagreement_pl_kernel(
         )
 
         wa = keep.tile([P, PASSES, N], U16, name="wa", align_bytes=64)
-        wb = keep.tile([P, PASSES, N], U32, name="wb", align_bytes=64)
+        wb = [keep.tile([P, N], U32, name="wb%d" % z, align_bytes=64) for z in range(PASSES)]
         ws = keep.tile([P, PASSES, N], U8, name="ws", align_bytes=64)
         nc.vector.tensor_copy(
             ws[:].rearrange("p z (t g i) -> p z g t i", t=PACK, i=16),
@@ -78,12 +77,14 @@ def tile_list_experts_disagreement_pl_kernel(
         )
         for z in range(PASSES):
             nc.vector.tensor_copy(
-                wb[:, z, :].rearrange("p (t g i) -> p g t i", t=PACK, i=4),
-                wb_raw[:, z, :].rearrange("p (g i t) -> p g t i", t=PACK, i=4),
-            )
-            nc.vector.tensor_copy(
                 wa[:, z, :].rearrange("p (t g i) -> p g t i", t=PACK, i=8),
                 wa_raw[:, z, :].rearrange("p (g i t) -> p g t i", t=PACK, i=8),
+            )
+
+        def deal_b(copy, z):
+            copy(
+                wb[z][:].rearrange("p (t g i) -> p g t i", t=PACK, i=4),
+                wb_raw[z][:].rearrange("p (g i t) -> p g t i", t=PACK, i=4),
             )
 
         def weave(dst, src):
@@ -91,22 +92,28 @@ def tile_list_experts_disagreement_pl_kernel(
                 dst.rearrange("p (c i t) -> p c t i", t=PACK, i=4), src.rearrange("p t (c i) -> p c t i", i=4)
             )
 
-        p_bank = [psum.tile([P, PACK, CH], F32, name="p%d" % c, tag="p%d" % c) for c in range(CHUNKS)]
-        q_bank = [psum.tile([P, PACK, CH], F32, name="q%d" % c, tag="q%d" % c) for c in range(CHUNKS)]
+        p_bank = [psum.tile([P, 2, HALF], F32, name="p%d" % n, tag="p%d" % n) for n in range(UNITS)]
+        q_bank = [psum.tile([P, 2, HALF], F32, name="q%d" % n, tag="q%d" % n) for n in range(UNITS)]
 
-        def products(z, c, codes, scales):
-            for bank, w, fmt, row0 in ((q_bank[c], wb, FP8X4, B_ROW), (p_bank[c], wa, FP4X4, 0)):
-                for t in range(PACK):
-                    cols = slice(t * P, (t + 1) * P)
-                    nc.tensor.matmul_mx(
-                        out=bank[:, t, :],
-                        lhsT=w[:, z, cols].bitcast(fmt),
-                        lhsT_scale=ws[row0:P, z, cols],
-                        rhs=codes.bitcast(FP8X4),
-                        rhs_scale=scales,
-                        start=(z == 0 and t == 0),
-                        stop=(z == PASSES - 1 and t == PACK - 1),
-                    )
+        def product(bank, w, fmt, row0, z, n, codes, scales):
+            for e in range(2):
+                t = 2 * (n % 2) + e
+                cols = slice(t * P, (t + 1) * P)
+                nc.tensor.matmul_mx(
+                    out=bank[:, e, :],
+                    lhsT=w[:, cols].bitcast(fmt),
+                    lhsT_scale=ws[row0:P, z, cols],
+                    rhs=codes.bitcast(FP8X4),
+                    rhs_scale=scales,
+                    start=(z == 0 and e == 0),
+                    stop=(z == PASSES - 1 and e == 1),
+                )
+
+        def product_a(z, n, codes, scales):
+            product(p_bank[n], wa[:, z, :], FP4X4, 0, z, n, codes, scales)
+
+        def product_b(z, n, codes, scales):
+            product(q_bank[n], wb[z][:], FP8X4, B_ROW, z, n, codes, scales)
 
         xg0 = keep.tile([P, PACK, J], BF16, name="xg0")
         for t in range(PACK):
@@ -116,89 +123,102 @@ def tile_list_experts_disagreement_pl_kernel(
         xc0 = keep.tile([P, J], U32, name="xc0", align_bytes=64)
         xs0 = keep.tile([P, J], U8, name="xs0", align_bytes=64)
         nc.vector.quantize_mx(out=xc0[:].bitcast(FP8X4), scales=xs0[:], in_=xw0[:])
-        for c in range(CHUNKS):
-            cols = slice(c * CH, (c + 1) * CH)
-            products(0, c, xc0[:, cols], xs0[:, cols])
+        deal_b(nc.vector.tensor_copy, 0)
+        for prod in (product_a, product_b):
+            for n in range(UNITS):
+                cols = slice(n // 2 * HALF, (n // 2 + 1) * HALF)
+                prod(0, n, xc0[:, cols], xs0[:, cols])
 
-        xg1 = [keep.tile([P, PACK, CH], BF16, name="xg1_%d" % c) for c in range(CHUNKS)]
+        xw1 = [keep.tile([P, HALF * PACK], BF16, name="xw1_%d" % h, align_bytes=64) for h in range(2)]
+        xg1 = keep.tile([P, PACK, HALF], BF16, name="xg1")
         for t in range(PACK):
-            for c in range(CHUNKS):
-                nc.scalar.activation(
-                    xg1[c][:, t, :], x_sb[1][t][:].indirect(offsets[:, c * CH // 16 : (c + 1) * CH // 16]), COPY
-                )
-        for c in range(CHUNKS):
-            xw = keep.tile([P, CH * PACK], BF16, name="xw1_%d" % c, align_bytes=64)
-            weave(xw[:], xg1[c][:])
-            xc = keep.tile([P, CH], U32, name="xc1_%d" % c, align_bytes=64)
-            xs = keep.tile([P, CH], U8, name="xs1_%d" % c, align_bytes=64)
-            nc.vector.quantize_mx(out=xc[:].bitcast(FP8X4), scales=xs[:], in_=xw[:])
-            products(1, c, xc[:], xs[:])
+            nc.vector.tensor_copy(
+                xw1[0][:].rearrange("p (j t) -> p t j", t=PACK)[:, t, :],
+                x_sb[1][t][:].indirect(offsets[:, 0 : HALF // 16]),
+            )
+            nc.scalar.activation(xg1[:, t, :], x_sb[1][t][:].indirect(offsets[:, HALF // 16 : J // 16]), COPY)
+        deal_b(nc.scalar.copy, 1)
+        for h in range(2):
+            if h == 1:
+                weave(xw1[1][:], xg1[:])
+            xc = keep.tile([P, HALF], U32, name="xc1_%d" % h, align_bytes=64)
+            xs = keep.tile([P, HALF], U8, name="xs1_%d" % h, align_bytes=64)
+            nc.vector.quantize_mx(out=xc[:].bitcast(FP8X4), scales=xs[:], in_=xw1[h][:])
+            for n in (2 * h, 2 * h + 1):
+                product_a(1, n, xc[:], xs[:])
+                product_b(1, n, xc[:], xs[:])
 
         y_rows = out_0.rearrange("(p t) j -> p t j", t=PACK)
         y_words = out_1[0].rearrange("p c r -> p (c r)").bitcast(I32)
         yc = keep.tile([P, J], U32, name="yc", align_bytes=64)
         ys = keep.tile([P, J], U8, name="ys", align_bytes=64)
-        LAST = CHUNKS - 1
-        pb = [bank[:].rearrange("p t j -> p (t j)") for bank in p_bank]
-        qb = [bank[:].rearrange("p t j -> p (t j)") for bank in q_bank]
-        qs = [keep.tile([P, PACK * CH], F32, name="qs%d" % c) for c in range(CHUNKS)]
-        low = [keep.tile([P, PACK * CH], F32, name="low%d" % c) for c in range(CHUNKS)]
-        part = [keep.tile([P, PACK * CH], F32, name="part%d" % c) for c in range(CHUNKS)]
-        u = [keep.tile([P, PACK, CH], F32, name="u%d" % c) for c in range(CHUNKS)]
-        y = [keep.tile([P, PACK, CH], F32, name="y%d" % c) for c in range(CHUNKS)]
-        yw = keep.tile([P, J * PACK], BF16, name="yw", align_bytes=64)
+        LAST = UNITS - 1
+        ps = [keep.tile([P, 2, HALF], F32, name="ps%d" % n) for n in range(UNITS)]
+        low = [keep.tile([P, 2, HALF], F32, name="low%d" % n) for n in range(UNITS)]
+        part = [keep.tile([P, 2, HALF], F32, name="part%d" % n) for n in range(UNITS)]
+        u = [keep.tile([P, 2, HALF], F32, name="u%d" % n) for n in range(UNITS)]
+        y = [keep.tile([P, 2, HALF], F32, name="y%d" % n) for n in range(UNITS)]
+        yw = [keep.tile([P, HALF * PACK], BF16, name="yw%d" % h, align_bytes=64) for h in range(2)]
+        whole = slice(0, HALF)
+        pieces = (slice(0, HALF // 2), slice(HALF // 2, HALF))
 
-        def step1(c):
-            nc.scalar.copy(qs[c][:], qb[c])
-            nc.vector.tensor_tensor(low[c][:], pb[c], qs[c][:], ALU.min)
+        def step0(n, js):
+            nc.scalar.copy(ps[n][:, :, js], p_bank[n][:, :, js])
 
-        def step2(c):
-            nc.vector.scalar_tensor_tensor(part[c][:], low[c][:], 2.0, pb[c], ALU.mult, ALU.add)
+        def step1(n, js):
+            nc.vector.tensor_tensor(low[n][:, :, js], q_bank[n][:, :, js], ps[n][:, :, js], ALU.min)
 
-        def step3(c):
-            nc.vector.tensor_tensor(u[c][:].rearrange("p t j -> p (t j)"), part[c][:], qb[c], ALU.add)
-
-        def gate(eng, c, a, b):
-            g = g4[:, c * CH + a : c * CH + b].unsqueeze(1).to_broadcast([P, PACK, b - a])
-            eng.tensor_tensor(y[c][:, :, a:b], u[c][:, :, a:b], g, ALU.mult)
-
-        def finish(c):
-            gate(nc.gpsimd, c, 0, CH)
-            nc.sync.dma_start(y_rows[:, :, c * CH : (c + 1) * CH], y[c][:])
-            nc.scalar.copy(
-                yw[:, c * CH * PACK : (c + 1) * CH * PACK].rearrange("p (c i t) -> p c t i", t=PACK, i=4),
-                y[c][:].rearrange("p t (c i) -> p c t i", i=4),
+        def step2(n, js):
+            nc.vector.scalar_tensor_tensor(
+                part[n][:, :, js], low[n][:, :, js], 2.0, q_bank[n][:, :, js], ALU.mult, ALU.add
             )
 
-        def planes(a, b):
-            nc.vector.quantize_mx(out=yc[:, a:b].bitcast(FP8X4), scales=ys[:, a:b], in_=yw[:, a * PACK : b * PACK])
+        def step3(n, js):
+            nc.vector.tensor_tensor(u[n][:, :, js], part[n][:, :, js], p_bank[n][:, :, js], ALU.add)
 
-        step1(0)
-        step1(1)
-        step2(0)
-        step2(1)
-        step3(0)
-        finish(0)
-        step1(2)
-        step3(1)
-        finish(1)
-        step2(2)
-        step1(3)
-        step3(2)
-        finish(2)
-        step2(3)
-        step3(3)
-        H = CH // 2
-        j0 = LAST * CH
-        for a in (0, H):
-            gate(nc.vector, LAST, a, a + H)
-        nc.sync.dma_start(y_rows[:, :, j0:J], y[LAST][:])
-        for a in (0, H):
-            weave(yw[:, (j0 + a) * PACK : (j0 + a + H) * PACK], y[LAST][:, :, a : a + H])
-        planes(0, j0)
-        nc.sync.dma_start(y_words[:, 0:j0], yc[:, 0:j0].bitcast(I32))
-        planes(j0, J)
-        nc.sync.dma_start(y_words[:, j0:J], yc[:, j0:J].bitcast(I32))
+        def gate(eng, n, js):
+            j0 = n // 2 * HALF
+            g = g4[:, j0 + js.start : j0 + js.stop].unsqueeze(1).to_broadcast([P, 2, js.stop - js.start])
+            eng.tensor_tensor(y[n][:, :, js], u[n][:, :, js], g, ALU.mult)
+
+        def store_y(n):
+            j0, t0 = n // 2 * HALF, 2 * (n % 2)
+            nc.sync.dma_start(y_rows[:, t0 : t0 + 2, j0 : j0 + HALF], y[n][:])
+
+        def weave_pair(copy, n, js):
+            t0 = 2 * (n % 2)
+            dst = yw[n // 2][:, js.start * PACK : js.stop * PACK].rearrange("p (c i t) -> p c t i", t=PACK, i=4)
+            copy(dst[:, :, t0 : t0 + 2, :], y[n][:, :, js].rearrange("p t (c i) -> p c t i", i=4))
+
+        def finish(n):
+            gate(nc.gpsimd, n, whole)
+            store_y(n)
+            weave_pair(nc.scalar.copy, n, whole)
+
+        def planes(h, js):
+            cols = slice(h * HALF + js.start, h * HALF + js.stop)
+            nc.vector.quantize_mx(
+                out=yc[:, cols].bitcast(FP8X4), scales=ys[:, cols], in_=yw[h][:, js.start * PACK : js.stop * PACK]
+            )
+
+        for n in range(UNITS):
+            for js in pieces if n == 0 else (whole,):
+                step0(n, js)
+            for step in (step1, step2, step3):
+                for js in pieces:
+                    step(n, js)
+            if n < LAST:
+                finish(n)
+        for js in pieces:
+            gate(nc.vector, LAST, js)
+        store_y(LAST)
+        planes(0, whole)
+        nc.sync.dma_start(y_words[:, 0:HALF], yc[:, 0:HALF].bitcast(I32))
+        for js in pieces:
+            weave_pair(nc.vector.tensor_copy, LAST, js)
+        for js in pieces:
+            planes(1, js)
+        nc.sync.dma_start(y_words[:, HALF:J], yc[:, HALF:J].bitcast(I32))
         for quad in range(4):
             queue = nc.scalar if quad % 2 == 0 else nc.sync
             queue.dma_start(

@@ -157,7 +157,7 @@ def tile_list_experts_disagreement_pl_kernel(
         low = [keep.tile([P, 2, HALF], F32, name="low%d" % n) for n in range(UNITS)]
         part = [keep.tile([P, 2, HALF], F32, name="part%d" % n) for n in range(UNITS)]
         u = [keep.tile([P, 2, HALF], F32, name="u%d" % n) for n in range(UNITS)]
-        y = [keep.tile([P, 2, HALF], F32, name="y%d" % n) for n in range(UNITS)]
+        y = {n: keep.tile([P, 2, HALF], F32, name="y%d" % n) for n in (0, 1, 3)}
         yw = [keep.tile([P, HALF * PACK], BF16, name="yw%d" % h, align_bytes=64) for h in range(2)]
         whole = slice(0, HALF)
         pieces = (slice(0, HALF // 2), slice(HALF // 2, HALF))
@@ -201,14 +201,26 @@ def tile_list_experts_disagreement_pl_kernel(
                 out=yc[:, cols].bitcast(FP8X4), scales=ys[:, cols], in_=yw[h][:, js.start * PACK : js.stop * PACK]
             )
 
-        for n in range(UNITS):
-            for js in pieces if n == 0 else (whole,):
-                step0(n, js)
-            for step in (step1, step2, step3):
+        def steps(n, which):
+            for step in which:
                 for js in pieces:
                     step(n, js)
-            if n < LAST:
-                finish(n)
+
+        steps(0, (step0, step1, step2))
+        nc.gpsimd.tensor_tensor(u[0][:], part[0][:], ps[0][:], ALU.add)
+        finish(0)
+        step0(1, whole)
+        steps(1, (step1, step2, step3))
+        finish(1)
+        step0(2, whole)
+        steps(2, (step1, step2, step3))
+        step0(3, whole)
+        steps(3, (step1, step2))
+        y[2] = keep.tile([P, 2, HALF], F32, name="y2", tag="u1")
+        gate(nc.vector, 2, whole)
+        store_y(2)
+        weave_pair(nc.scalar.copy, 2, whole)
+        steps(3, (step3,))
         for js in pieces:
             gate(nc.vector, LAST, js)
         store_y(LAST)

@@ -22,6 +22,8 @@ PACK = 4
 PASSES = K // (P * PACK)
 HALF = J // 2
 UNITS = 4
+SUMMED = (0, 1)
+ABS = mybir.ActivationFunctionType.Abs
 B_ROW = 4
 
 
@@ -87,15 +89,13 @@ def tile_list_experts_disagreement_pl_kernel(
                 wb_raw[z][:].rearrange("p (g i t) -> p g t i", t=PACK, i=4),
             )
 
-        def weave(dst, src):
-            nc.vector.tensor_copy(
-                dst.rearrange("p (c i t) -> p c t i", t=PACK, i=4), src.rearrange("p t (c i) -> p c t i", i=4)
-            )
+        def weave(copy, dst, src):
+            copy(dst.rearrange("p (c i t) -> p c t i", t=PACK, i=4), src.rearrange("p t (c i) -> p c t i", i=4))
 
         p_bank = [psum.tile([P, 2, HALF], F32, name="p%d" % n, tag="p%d" % n) for n in range(UNITS)]
         q_bank = [psum.tile([P, 2, HALF], F32, name="q%d" % n, tag="q%d" % n) for n in range(UNITS)]
 
-        def product(bank, w, fmt, row0, z, n, codes, scales):
+        def product(bank, w, fmt, row0, z, n, codes, scales, first, last):
             for e in range(2):
                 t = 2 * (n % 2) + e
                 cols = slice(t * P, (t + 1) * P)
@@ -105,29 +105,32 @@ def tile_list_experts_disagreement_pl_kernel(
                     lhsT_scale=ws[row0:P, z, cols],
                     rhs=codes.bitcast(FP8X4),
                     rhs_scale=scales,
-                    start=(z == 0 and e == 0),
-                    stop=(z == PASSES - 1 and e == 1),
+                    start=(first and e == 0),
+                    stop=(last and e == 1),
                 )
 
-        def product_a(z, n, codes, scales):
-            product(p_bank[n], wa[:, z, :], FP4X4, 0, z, n, codes, scales)
+        def product_a(bank, z, n, codes, scales, first, last):
+            product(bank, wa[:, z, :], FP4X4, 0, z, n, codes, scales, first, last)
 
-        def product_b(z, n, codes, scales):
-            product(q_bank[n], wb[z][:], FP8X4, B_ROW, z, n, codes, scales)
+        def product_b(bank, z, n, codes, scales, first, last):
+            product(bank, wb[z][:], FP8X4, B_ROW, z, n, codes, scales, first, last)
 
         xg0 = keep.tile([P, PACK, J], BF16, name="xg0")
         for t in range(PACK):
             nc.scalar.activation(xg0[:, t, :], x_sb[0][t][:].indirect(offsets[:]), COPY)
         xw0 = keep.tile([P, J * PACK], BF16, name="xw0", align_bytes=64)
-        weave(xw0[:], xg0[:])
+        weave(nc.vector.tensor_copy, xw0[:], xg0[:])
         xc0 = keep.tile([P, J], U32, name="xc0", align_bytes=64)
         xs0 = keep.tile([P, J], U8, name="xs0", align_bytes=64)
         nc.vector.quantize_mx(out=xc0[:].bitcast(FP8X4), scales=xs0[:], in_=xw0[:])
         deal_b(nc.vector.tensor_copy, 0)
-        for prod in (product_a, product_b):
-            for n in range(UNITS):
-                cols = slice(n // 2 * HALF, (n // 2 + 1) * HALF)
-                prod(0, n, xc0[:, cols], xs0[:, cols])
+        x0 = [(xc0[:, h * HALF : (h + 1) * HALF], xs0[:, h * HALF : (h + 1) * HALF]) for h in range(2)]
+        for n in range(UNITS):
+            product_a(p_bank[n], 0, n, *x0[n // 2], True, False)
+        for n in SUMMED:
+            product_a(q_bank[n], 0, n, *x0[n // 2], True, False)
+        for n in range(UNITS):
+            product_b(q_bank[n], 0, n, *x0[n // 2], n not in SUMMED, False)
 
         xw1 = [keep.tile([P, HALF * PACK], BF16, name="xw1_%d" % h, align_bytes=64) for h in range(2)]
         xg1 = keep.tile([P, PACK, HALF], BF16, name="xg1")
@@ -140,13 +143,15 @@ def tile_list_experts_disagreement_pl_kernel(
         deal_b(nc.scalar.copy, 1)
         for h in range(2):
             if h == 1:
-                weave(xw1[1][:], xg1[:])
+                weave(nc.vector.tensor_copy, xw1[1][:], xg1[:])
             xc = keep.tile([P, HALF], U32, name="xc1_%d" % h, align_bytes=64)
             xs = keep.tile([P, HALF], U8, name="xs1_%d" % h, align_bytes=64)
             nc.vector.quantize_mx(out=xc[:].bitcast(FP8X4), scales=xs[:], in_=xw1[h][:])
             for n in (2 * h, 2 * h + 1):
-                product_a(1, n, xc[:], xs[:])
-                product_b(1, n, xc[:], xs[:])
+                product_a(p_bank[n], 1, n, xc[:], xs[:], False, True)
+                product_b(q_bank[n], 1, n, xc[:], xs[:], False, n not in SUMMED)
+                if n in SUMMED:
+                    product_a(q_bank[n], 1, n, xc[:], xs[:], False, True)
 
         y_rows = out_0.rearrange("(p t) j -> p t j", t=PACK)
         y_words = out_1[0].rearrange("p c r -> p (c r)").bitcast(I32)
@@ -157,7 +162,7 @@ def tile_list_experts_disagreement_pl_kernel(
         low = [keep.tile([P, 2, HALF], F32, name="low%d" % n) for n in range(UNITS)]
         part = [keep.tile([P, 2, HALF], F32, name="part%d" % n) for n in range(UNITS)]
         u = [keep.tile([P, 2, HALF], F32, name="u%d" % n) for n in range(UNITS)]
-        y = {n: keep.tile([P, 2, HALF], F32, name="y%d" % n) for n in (0, 1, 3)}
+        y = [keep.tile([P, PACK, HALF], F32, name="y0")]
         yw = [keep.tile([P, HALF * PACK], BF16, name="yw%d" % h, align_bytes=64) for h in range(2)]
         whole = slice(0, HALF)
         pieces = (slice(0, HALF // 2), slice(HALF // 2, HALF))
@@ -177,23 +182,20 @@ def tile_list_experts_disagreement_pl_kernel(
             nc.vector.tensor_tensor(u[n][:, :, js], part[n][:, :, js], p_bank[n][:, :, js], ALU.add)
 
         def gate(eng, n, js):
-            j0 = n // 2 * HALF
+            j0, t0 = n // 2 * HALF, 2 * (n % 2)
             g = g4[:, j0 + js.start : j0 + js.stop].unsqueeze(1).to_broadcast([P, 2, js.stop - js.start])
-            eng.tensor_tensor(y[n][:, :, js], u[n][:, :, js], g, ALU.mult)
+            eng.tensor_tensor(y[n // 2][:, t0 : t0 + 2, js], u[n][:, :, js], g, ALU.mult)
 
         def store_y(n):
             j0, t0 = n // 2 * HALF, 2 * (n % 2)
-            nc.sync.dma_start(y_rows[:, t0 : t0 + 2, j0 : j0 + HALF], y[n][:])
+            nc.sync.dma_start(y_rows[:, t0 : t0 + 2, j0 : j0 + HALF], y[n // 2][:, t0 : t0 + 2, :])
 
-        def weave_pair(copy, n, js):
-            t0 = 2 * (n % 2)
-            dst = yw[n // 2][:, js.start * PACK : js.stop * PACK].rearrange("p (c i t) -> p c t i", t=PACK, i=4)
-            copy(dst[:, :, t0 : t0 + 2, :], y[n][:, :, js].rearrange("p t (c i) -> p c t i", i=4))
+        def weave_y(copy, h, js):
+            weave(copy, yw[h][:, js.start * PACK : js.stop * PACK], y[h][:, :, js])
 
         def finish(n):
             gate(nc.gpsimd, n, whole)
             store_y(n)
-            weave_pair(nc.scalar.copy, n, whole)
 
         def planes(h, js):
             cols = slice(h * HALF + js.start, h * HALF + js.stop)
@@ -206,28 +208,37 @@ def tile_list_experts_disagreement_pl_kernel(
                 for js in pieces:
                     step(n, js)
 
-        steps(0, (step0, step1, step2))
-        nc.gpsimd.tensor_tensor(u[0][:], part[0][:], ps[0][:], ALU.add)
-        finish(0)
+        def diff(n, js):
+            nc.vector.scalar_tensor_tensor(
+                low[n][:, :, js], ps[n][:, :, js], -2.0, q_bank[n][:, :, js], ALU.mult, ALU.add
+            )
+            nc.scalar.activation(part[n][:, :, js], low[n][:, :, js], ABS)
+
+        def join(n, js):
+            nc.vector.scalar_tensor_tensor(
+                u[n][:, :, js], q_bank[n][:, :, js], 2.0, part[n][:, :, js], ALU.mult, ALU.subtract
+            )
+
+        steps(0, (step0, diff))
         step0(1, whole)
-        steps(1, (step1, step2, step3))
-        finish(1)
-        step0(2, whole)
-        steps(2, (step1, step2, step3))
-        step0(3, whole)
-        steps(3, (step1, step2))
-        y[2] = keep.tile([P, 2, HALF], F32, name="y2", tag="u1")
-        gate(nc.vector, 2, whole)
-        store_y(2)
-        weave_pair(nc.scalar.copy, 2, whole)
-        steps(3, (step3,))
+        steps(1, (diff,))
+        for n in SUMMED:
+            steps(n, (join,))
+            finish(n)
+        weave_y(nc.scalar.copy, 0, whole)
+        y.append(keep.tile([P, PACK, HALF], F32, name="y1"))
+        for n in (2, 3):
+            step0(n, whole)
+            steps(n, (step1, step2, step3))
+            if n < LAST:
+                finish(n)
         for js in pieces:
             gate(nc.vector, LAST, js)
         store_y(LAST)
         planes(0, whole)
         nc.sync.dma_start(y_words[:, 0:HALF], yc[:, 0:HALF].bitcast(I32))
-        for js in pieces:
-            weave_pair(nc.vector.tensor_copy, LAST, js)
+        weave_y(nc.scalar.copy, 1, pieces[0])
+        weave_y(nc.vector.tensor_copy, 1, pieces[1])
         for js in pieces:
             planes(1, js)
         nc.sync.dma_start(y_words[:, HALF:J], yc[:, HALF:J].bitcast(I32))

@@ -46,21 +46,19 @@ def tile_list_experts_disagreement_pl_kernel(
 
         nc.vector.memset(ws_raw[:].bitcast(I32), 0)
         make_identity(nc, ident[:])
-        small = [(offsets[:], offs), (ga_col[:], ga[0].rearrange("(p c) -> p c", c=PACK))]
         for quad in range(4):
             for row0, src in ((0, wa_scales), (B_ROW, wb_scales)):
-                small.append((
+                nc.gpsimd.dma_start(
                     ws_raw[32 * quad + row0 : 32 * quad + row0 + 4].bitcast(I32),
                     src[:, 4 * quad : 4 * quad + 4, :].rearrange("z q c -> q z c").bitcast(I32),
-                ))
+                )
+        nc.gpsimd.dma_start(ga_col[:], ga[0].rearrange("(p c) -> p c", c=PACK))
         big = [(x_sb[z][t][:], x_rows[z, t]) for z in range(PASSES) for t in range(PACK)]
         wb_load = [(wb_raw[z][:].bitcast(I32), wb_words[z].rearrange("p c r -> p (c r)").bitcast(I32)) for z in range(PASSES)]
         wa_load = (wa_raw[:].bitcast(I32), wa_words.rearrange("z p b -> p z b").bitcast(I32))
-        big = big[:6] + [wa_load, big[6], wb_load[0], big[7], wb_load[1]]
-        for i, (dst, src) in enumerate(big):
+        big = [big[0], (offsets[:], offs)] + big[1:6] + [wa_load, big[6], wb_load[0], big[7], wb_load[1]]
+        for dst, src in big:
             nc.sync.dma_start(dst, src)
-            for dst, src in small[2 * i : 2 * i + 2]:
-                nc.sync.dma_start(dst, src)
 
         g_bank = psum.tile([P, PACK, P], F32, name="g_bank", tag="q%d" % (UNITS - 1))
         for c in range(PACK):
@@ -149,9 +147,9 @@ def tile_list_experts_disagreement_pl_kernel(
             nc.vector.quantize_mx(out=xc[:].bitcast(FP8X4), scales=xs[:], in_=xw1[h][:])
             for n in (2 * h, 2 * h + 1):
                 product_a(p_bank[n], 1, n, xc[:], xs[:], False, True)
-                product_b(q_bank[n], 1, n, xc[:], xs[:], False, n not in SUMMED)
                 if n in SUMMED:
-                    product_a(q_bank[n], 1, n, xc[:], xs[:], False, True)
+                    product_a(q_bank[n], 1, n, xc[:], xs[:], False, False)
+                product_b(q_bank[n], 1, n, xc[:], xs[:], False, True)
 
         y_rows = out_0.rearrange("(p t) j -> p t j", t=PACK)
         y_words = out_1[0].rearrange("p c r -> p (c r)").bitcast(I32)

from contextlib import ExitStack

import concourse.mybir as mybir
from concourse.masks import make_identity

K, T, J, N = 1024, 2048, 512, 512
FLOPS = 2 * 2 * K * J * N

F32 = mybir.dt.float32
BF16 = mybir.dt.bfloat16
I32 = mybir.dt.int32
U32 = mybir.dt.uint32
U16 = mybir.dt.uint16
U8 = mybir.dt.uint8
FP8X4 = mybir.dt.float8_e4m3fn_x4
FP4X4 = mybir.dt.float4_e2m1fn_x4
ALU = mybir.AluOpType
COPY = mybir.ActivationFunctionType.Copy

P = 128
PACK = 4
PASSES = K // (P * PACK)
HALF = J // 2
UNITS = 4
SUMMED = (0, 1)
ABS = mybir.ActivationFunctionType.Abs
B_ROW = 4


def tile_list_experts_disagreement_pl_kernel(
    tc, xq, wa_words, wa_scales, wb_words, wb_scales, ga, offs, out_0, out_1, out_2
):
    nc = tc.nc
    with ExitStack() as ctx:
        keep = ctx.enter_context(tc.tile_pool(name="keep", bufs=1))
        psum = ctx.enter_context(tc.psum_pool(name="psum", bufs=1))

        x_rows = xq.rearrange("(z p t) c -> z t p c", p=P, t=PACK)
        x_sb = [[keep.tile([P, T], F32, name="x%d%d" % (z, t)) for t in range(PACK)] for z in range(PASSES)]
        offsets = keep.tile([P, J // 16], U16, name="offsets")
        wa_raw = keep.tile([P, PASSES, N], U16, name="wa_raw")
        wb_raw = [keep.tile([P, N], U32, name="wb_raw%d" % z) for z in range(PASSES)]
        ws_raw = keep.tile([P, PASSES, N], U8, name="ws_raw")
        ga_col = keep.tile([P, PACK], F32, name="ga_col")
        ident = keep.tile([P, P], F32, name="ident")

        nc.vector.memset(ws_raw[:].bitcast(I32), 0)
        make_identity(nc, ident[:])
        for quad in range(4):
            for row0, src in ((0, wa_scales), (B_ROW, wb_scales)):
                nc.gpsimd.dma_start(
                    ws_raw[32 * quad + row0 : 32 * quad + row0 + 4].bitcast(I32),
                    src[:, 4 * quad : 4 * quad + 4, :].rearrange("z q c -> q z c").bitcast(I32),
                )
        nc.gpsimd.dma_start(ga_col[:], ga[0].rearrange("(p c) -> p c", c=PACK))
        big = [(x_sb[z][t][:], x_rows[z, t]) for z in range(PASSES) for t in range(PACK)]
        wb_load = [(wb_raw[z][:].bitcast(I32), wb_words[z].rearrange("p c r -> p (c r)").bitcast(I32)) for z in range(PASSES)]
        wa_load = (wa_raw[:].bitcast(I32), wa_words.rearrange("z p b -> p z b").bitcast(I32))
        big = [big[0], (offsets[:], offs)] + big[1:6] + [wa_load, big[6], wb_load[0], big[7], wb_load[1]]
        for dst, src in big:
            nc.sync.dma_start(dst, src)

        g_bank = psum.tile([P, PACK, P], F32, name="g_bank", tag="q%d" % (UNITS - 1))
        for c in range(PACK):
            nc.tensor.transpose(g_bank[:, c, :], ga_col[:, c : c + 1].to_broadcast([P, P]), ident[:])
        g4 = keep.tile([P, J], F32, name="g4")
        nc.vector.tensor_scalar(
            g4[:].rearrange("p (m c) -> p m c", c=PACK), g_bank[:].rearrange("p c m -> p m c"), 0.25, None, ALU.mult
        )

        wa = keep.tile([P, PASSES, N], U16, name="wa", align_bytes=64)
        wb = [keep.tile([P, N], U32, name="wb%d" % z, align_bytes=64) for z in range(PASSES)]
        ws = keep.tile([P, PASSES, N], U8, name="ws", align_bytes=64)
        nc.vector.tensor_copy(
            ws[:].rearrange("p z (t g i) -> p z g t i", t=PACK, i=16),
            ws_raw[:].rearrange("p z (g i t) -> p z g t i", t=PACK, i=16),
        )
        for z in range(PASSES):
            nc.vector.tensor_copy(
                wa[:, z, :].rearrange("p (t g i) -> p g t i", t=PACK, i=8),
                wa_raw[:, z, :].rearrange("p (g i t) -> p g t i", t=PACK, i=8),
            )

        def deal_b(copy, z):
            copy(
                wb[z][:].rearrange("p (t g i) -> p g t i", t=PACK, i=4),
                wb_raw[z][:].rearrange("p (g i t) -> p g t i", t=PACK, i=4),
            )

        def weave(copy, dst, src):
            copy(dst.rearrange("p (c i t) -> p c t i", t=PACK, i=4), src.rearrange("p t (c i) -> p c t i", i=4))

        p_bank = [psum.tile([P, 2, HALF], F32, name="p%d" % n, tag="p%d" % n) for n in range(UNITS)]
        q_bank = [psum.tile([P, 2, HALF], F32, name="q%d" % n, tag="q%d" % n) for n in range(UNITS)]

        def product(bank, w, fmt, row0, z, n, codes, scales, first, last):
            for e in range(2):
                t = 2 * (n % 2) + e
                cols = slice(t * P, (t + 1) * P)
                nc.tensor.matmul_mx(
                    out=bank[:, e, :],
                    lhsT=w[:, cols].bitcast(fmt),
                    lhsT_scale=ws[row0:P, z, cols],
                    rhs=codes.bitcast(FP8X4),
                    rhs_scale=scales,
                    start=(first and e == 0),
                    stop=(last and e == 1),
                )

        def product_a(bank, z, n, codes, scales, first, last):
            product(bank, wa[:, z, :], FP4X4, 0, z, n, codes, scales, first, last)

        def product_b(bank, z, n, codes, scales, first, last):
            product(bank, wb[z][:], FP8X4, B_ROW, z, n, codes, scales, first, last)

        xg0 = keep.tile([P, PACK, J], BF16, name="xg0")
        for t in range(PACK):
            nc.scalar.activation(xg0[:, t, :], x_sb[0][t][:].indirect(offsets[:]), COPY)
        xw0 = keep.tile([P, J * PACK], BF16, name="xw0", align_bytes=64)
        weave(nc.vector.tensor_copy, xw0[:], xg0[:])
        xc0 = keep.tile([P, J], U32, name="xc0", align_bytes=64)
        xs0 = keep.tile([P, J], U8, name="xs0", align_bytes=64)
        nc.vector.quantize_mx(out=xc0[:].bitcast(FP8X4), scales=xs0[:], in_=xw0[:])
        deal_b(nc.vector.tensor_copy, 0)
        x0 = [(xc0[:, h * HALF : (h + 1) * HALF], xs0[:, h * HALF : (h + 1) * HALF]) for h in range(2)]
        for n in range(UNITS):
            product_a(p_bank[n], 0, n, *x0[n // 2], True, False)
        for n in SUMMED:
            product_a(q_bank[n], 0, n, *x0[n // 2], True, False)
        for n in range(UNITS):
            product_b(q_bank[n], 0, n, *x0[n // 2], n not in SUMMED, False)

        xw1 = [keep.tile([P, HALF * PACK], BF16, name="xw1_%d" % h, align_bytes=64) for h in range(2)]
        xg1 = keep.tile([P, PACK, HALF], BF16, name="xg1")
        for t in range(PACK):
            nc.vector.tensor_copy(
                xw1[0][:].rearrange("p (j t) -> p t j", t=PACK)[:, t, :],
                x_sb[1][t][:].indirect(offsets[:, 0 : HALF // 16]),
            )
            nc.scalar.activation(xg1[:, t, :], x_sb[1][t][:].indirect(offsets[:, HALF // 16 : J // 16]), COPY)
        deal_b(nc.scalar.copy, 1)
        for h in range(2):
            if h == 1:
                weave(nc.vector.tensor_copy, xw1[1][:], xg1[:])
            xc = keep.tile([P, HALF], U32, name="xc1_%d" % h, align_bytes=64)
            xs = keep.tile([P, HALF], U8, name="xs1_%d" % h, align_bytes=64)
            nc.vector.quantize_mx(out=xc[:].bitcast(FP8X4), scales=xs[:], in_=xw1[h][:])
            for n in (2 * h, 2 * h + 1):
                product_a(p_bank[n], 1, n, xc[:], xs[:], False, True)
                if n in SUMMED:
                    product_a(q_bank[n], 1, n, xc[:], xs[:], False, False)
                product_b(q_bank[n], 1, n, xc[:], xs[:], False, True)

        y_rows = out_0.rearrange("(p t) j -> p t j", t=PACK)
        y_words = out_1[0].rearrange("p c r -> p (c r)").bitcast(I32)
        yc = keep.tile([P, J], U32, name="yc", align_bytes=64)
        ys = keep.tile([P, J], U8, name="ys", align_bytes=64)
        LAST = UNITS - 1
        ps = [keep.tile([P, 2, HALF], F32, name="ps%d" % n) for n in range(UNITS)]
        low = [keep.tile([P, 2, HALF], F32, name="low%d" % n) for n in range(UNITS)]
        part = [keep.tile([P, 2, HALF], F32, name="part%d" % n) for n in range(UNITS)]
        u = [keep.tile([P, 2, HALF], F32, name="u%d" % n) for n in range(UNITS)]
        y = [keep.tile([P, PACK, HALF], F32, name="y0")]
        yw = [keep.tile([P, HALF * PACK], BF16, name="yw%d" % h, align_bytes=64) for h in range(2)]
        whole = slice(0, HALF)
        pieces = (slice(0, HALF // 2), slice(HALF // 2, HALF))

        def step0(n, js):
            nc.scalar.copy(ps[n][:, :, js], p_bank[n][:, :, js])

        def step1(n, js):
            nc.vector.tensor_tensor(low[n][:, :, js], q_bank[n][:, :, js], ps[n][:, :, js], ALU.min)

        def step2(n, js):
            nc.vector.scalar_tensor_tensor(
                part[n][:, :, js], low[n][:, :, js], 2.0, q_bank[n][:, :, js], ALU.mult, ALU.add
            )

        def step3(n, js):
            nc.vector.tensor_tensor(u[n][:, :, js], part[n][:, :, js], p_bank[n][:, :, js], ALU.add)

        def gate(eng, n, js):
            j0, t0 = n // 2 * HALF, 2 * (n % 2)
            g = g4[:, j0 + js.start : j0 + js.stop].unsqueeze(1).to_broadcast([P, 2, js.stop - js.start])
            eng.tensor_tensor(y[n // 2][:, t0 : t0 + 2, js], u[n][:, :, js], g, ALU.mult)

        def store_y(n):
            j0, t0 = n // 2 * HALF, 2 * (n % 2)
            nc.sync.dma_start(y_rows[:, t0 : t0 + 2, j0 : j0 + HALF], y[n // 2][:, t0 : t0 + 2, :])

        def weave_y(copy, h, js):
            weave(copy, yw[h][:, js.start * PACK : js.stop * PACK], y[h][:, :, js])

        def finish(n):
            gate(nc.gpsimd, n, whole)
            store_y(n)

        def planes(h, js):
            cols = slice(h * HALF + js.start, h * HALF + js.stop)
            nc.vector.quantize_mx(
                out=yc[:, cols].bitcast(FP8X4), scales=ys[:, cols], in_=yw[h][:, js.start * PACK : js.stop * PACK]
            )

        def steps(n, which):
            for step in which:
                for js in pieces:
                    step(n, js)

        def diff(n, js):
            nc.vector.scalar_tensor_tensor(
                low[n][:, :, js], ps[n][:, :, js], -2.0, q_bank[n][:, :, js], ALU.mult, ALU.add
            )
            nc.scalar.activation(part[n][:, :, js], low[n][:, :, js], ABS)

        def join(n, js):
            nc.vector.scalar_tensor_tensor(
                u[n][:, :, js], q_bank[n][:, :, js], 2.0, part[n][:, :, js], ALU.mult, ALU.subtract
            )

        steps(0, (step0, diff))
        step0(1, whole)
        steps(1, (diff,))
        for n in SUMMED:
            steps(n, (join,))
            finish(n)
        weave_y(nc.scalar.copy, 0, whole)
        y.append(keep.tile([P, PACK, HALF], F32, name="y1"))
        for n in (2, 3):
            step0(n, whole)
            steps(n, (step1, step2, step3))
            if n < LAST:
                finish(n)
        for js in pieces:
            gate(nc.vector, LAST, js)
        store_y(LAST)
        planes(0, whole)
        nc.sync.dma_start(y_words[:, 0:HALF], yc[:, 0:HALF].bitcast(I32))
        weave_y(nc.scalar.copy, 1, pieces[0])
        weave_y(nc.vector.tensor_copy, 1, pieces[1])
        for js in pieces:
            planes(1, js)
        nc.sync.dma_start(y_words[:, HALF:J], yc[:, HALF:J].bitcast(I32))
        for quad in range(4):
            queue = nc.scalar if quad % 2 == 0 else nc.sync
            queue.dma_start(
                out_2[0, 4 * quad : 4 * quad + 4, :].bitcast(I32), ys[32 * quad : 32 * quad + 4, :].bitcast(I32)
            )
